import numpy as np
import ml_dtypes


def mxq(x, axis, fmt="e4m3"):
    dtype, down = {"e4m3": (ml_dtypes.float8_e4m3fn, 7), "e5m2": (ml_dtypes.float8_e5m2, 14)}[fmt]
    v = np.moveaxis(np.asarray(x, np.float32).astype(ml_dtypes.bfloat16).astype(np.float64), axis, -1)
    blocks = v.reshape(v.shape[:-1] + (-1, 32))
    amax = np.abs(blocks).max(-1, keepdims=True)
    byte = np.maximum(np.where(amax > 0, np.frexp(amax)[1] - 1 + 127, 0) - down, 1)
    scale = np.exp2(byte - 127.0)
    codes = (blocks / scale).astype(np.float32).astype(dtype).astype(np.float64)
    return np.moveaxis((codes * scale).reshape(v.shape), -1, axis)


WIDE = False


def mx_kscale(k):
    if not WIDE:
        return np.ones(k)
    levels = np.array([10, -10, 5, -5, 0])
    if k % 512:
        return np.exp2(np.random.permutation(np.resize(levels, k // 32))).repeat(32)
    a = np.empty((k // 512, 16))
    for p in range(k // 512):
        a[p, :8] = np.random.permutation(np.resize(levels, 8))
        for g in range(8):
            far = levels[np.abs(levels - a[p, g]) >= 10]
            a[p, g + 8] = far[np.random.randint(len(far))]
    return np.exp2(a.ravel()).repeat(32)


def f64(x):
    return np.asarray(x).astype(np.float64)


E2M1 = np.array([0.0, 0.5, 1.0, 1.5, 2.0, 3.0, 4.0, 6.0, -0.0, -0.5, -1.0, -1.5, -2.0, -3.0, -4.0, -6.0])


def pack_weight(w, fmt):
    k, n = w.shape
    w = f64(np.asarray(w, np.float32).astype(ml_dtypes.bfloat16)).reshape(k // 32, 32, n)
    amax = np.abs(w).max(1)
    if fmt == "e4m3":
        byte = np.frexp(amax)[1] - 1 + 127 - 7
    else:
        mant, ex = np.frexp(amax / 6.0)
        byte = np.where(mant > 0.5, ex, ex - 1) + 127
    byte = np.clip(np.where(amax > 0, byte, 1), 1, 254)
    scaled = (w * np.exp2(127.0 - byte)[:, None, :]).reshape(k, n).astype(np.float32)
    by_word = np.ascontiguousarray(scaled.reshape(k // 512, 128, 4, n).transpose(0, 1, 3, 2))
    if fmt == "e4m3":
        words = by_word.astype(ml_dtypes.float8_e4m3fn).view(np.uint8)
    else:
        c = by_word.astype(ml_dtypes.float4_e2m1fn).view(np.uint8) & 0xF
        words = (c[..., 0::2] | (c[..., 1::2] << 4)).reshape(k // 512, 128, 2 * n)
    return np.ascontiguousarray(words), np.ascontiguousarray(byte.astype(np.uint8).reshape(k // 512, 16, n))


def unpack_weight(words, scales, fmt):
    g, _, n = scales.shape
    words = np.ascontiguousarray(words).reshape(g, 128, n, -1)
    if fmt == "e4m3":
        vals = words.view(ml_dtypes.float8_e4m3fn).astype(np.float64)
    else:
        nib = np.empty((g, 128, n, 4), np.uint8)
        nib[..., 0::2] = words & 0xF
        nib[..., 1::2] = words >> 4
        vals = E2M1[nib]
    vals = vals * np.repeat(np.exp2(scales.astype(np.float64) - 127.0), 8, axis=1)[..., None]
    return vals.transpose(0, 1, 3, 2).reshape(g * 512, n)


K, L, T, N = 512, 1024, 512, 512


def setup_inputs():
    n = np.random.standard_normal
    fk = mx_kscale(K)
    fl = mx_kscale(L)
    xtp = pack_weight(n((K, T)) / fk[:, None], "e4m3")
    wap = pack_weight(n((K, N)) * 1 / np.sqrt(K) * fk[:, None], "e2m1")
    wqp = pack_weight(n((L, N)) * 1 / np.sqrt(L) * fl[:, None], "e2m1")
    wbp = pack_weight(n((K, N)) * 1 / np.sqrt(K) * fk[:, None], "e4m3")
    wsp = pack_weight(n((L, N)) * 1 / np.sqrt(L) * fl[:, None], "e2m1")
    return {
        "xt_words": xtp[0],
        "xt_scales": xtp[1],
        "wa_words": wap[0],
        "wa_scales": wap[1],
        "xq": (n((L, T)) / fl[:, None]).astype(np.float32),
        "wq_words": wqp[0],
        "wq_scales": wqp[1],
        "wb_words": wbp[0],
        "wb_scales": wbp[1],
        "ws_words": wsp[0],
        "ws_scales": wsp[1],
    }


def reference(xt_words, xt_scales, wa_words, wa_scales, xq, wq_words, wq_scales, wb_words, wb_scales, ws_words, ws_scales):
    xtu = unpack_weight(xt_words, xt_scales, "e4m3")
    wau = unpack_weight(wa_words, wa_scales, "e2m1")
    wqu = unpack_weight(wq_words, wq_scales, "e2m1")
    wbu = unpack_weight(wb_words, wb_scales, "e4m3")
    wsu = unpack_weight(ws_words, ws_scales, "e2m1")
    xqq = mxq(f64(xq), 0, "e4m3")
    p = wau.T @ xtu + wqu.T @ xqq
    r = wbu.T @ xtu + wsu.T @ xqq
    y = p * r / (1.0 + np.abs(r))
    return y

@@ -1,0 +1,151 @@
+from contextlib import ExitStack
+
+import concourse.mybir as mybir
+
+K, L, T, N = 512, 1024, 512, 512
+FLOPS = 2 * 2 * (K + L) * T * N
+
+F32 = mybir.dt.float32
+BF16 = mybir.dt.bfloat16
+I32 = mybir.dt.int32
+U32 = mybir.dt.uint32
+U8 = mybir.dt.uint8
+FP8X4 = mybir.dt.float8_e4m3fn_x4
+FP4X4 = mybir.dt.float4_e2m1fn_x4
+ACT = mybir.ActivationFunctionType
+ALU = mybir.AluOpType
+
+P = 128
+PACK = 4
+PASS = P * PACK
+N_TILES = N // P
+HALF = T // 2
+QUARTER = T // 4
+
+
+def tile_mix_product_of_two_sums_kernel(
+    tc, xt_words, xt_scales, wa_words, wa_scales, xq, wq_words, wq_scales, wb_words, wb_scales, ws_words, ws_scales, out
+):
+    nc = tc.nc
+    with ExitStack() as ctx:
+        keep = ctx.enter_context(tc.tile_pool(name="keep", bufs=1))
+        psum = ctx.enter_context(tc.psum_pool(name="psum", bufs=1))
+        ctx.enter_context(tc.manual_schedule())
+
+        def plane_tile(name, passes):
+            plane = keep.tile([P, passes * N], U8, name=name, align_bytes=64)
+            nc.vector.memset(plane[:].bitcast(I32), 0)
+            return plane
+
+        def load_scales(plane, scales):
+            passes = scales.shape[0]
+            rows = scales.bitcast(I32).rearrange("z (q r) c -> r q z c", r=4)
+            for r in range(4):
+                nc.sync.dma_start(
+                    out=plane[:].bitcast(I32)[r:P:32, :].rearrange("q (z c) -> q z c", z=passes), in_=rows[r]
+                )
+
+        def load_words(name, words):
+            passes, width = words.shape[0], words.shape[2]
+            codes = keep.tile([P, passes * width], U8, name=name, align_bytes=64)
+            nc.sync.dma_start(
+                out=codes[:].bitcast(I32).rearrange("p (z c) -> p z c", z=passes),
+                in_=words.bitcast(I32).rearrange("z p c -> p z c"),
+            )
+            return codes
+
+        def load_xq(z, h):
+            raw = keep.tile([P, PACK, HALF], F32, name="xq_raw_%d_%d" % (z, h))
+            rows = xq[z * PASS : (z + 1) * PASS, h * HALF : (h + 1) * HALF]
+            nc.sync.dma_start(out=raw[:], in_=rows.rearrange("(p j) w -> p j w", j=PACK))
+            return raw
+
+
+        xt_plane = plane_tile("xt_plane", 1)
+        wb_plane = plane_tile("wb_plane", 1)
+        ws_plane = plane_tile("ws_plane", 2)
+        wa_plane = plane_tile("wa_plane", 1)
+        wq_plane = plane_tile("wq_plane", 2)
+
+        raw = {}
+        raw[0, 0] = load_xq(0, 0)
+        xt = load_words("xt", xt_words.rearrange("z p c r -> z p (c r)"))
+        wb = load_words("wb", wb_words.rearrange("z p c r -> z p (c r)"))
+        load_scales(xt_plane, xt_scales)
+        raw[0, 1] = load_xq(0, 1)
+        load_scales(wb_plane, wb_scales)
+        wa = load_words("wa", wa_words)
+        ws = load_words("ws", ws_words)
+        raw[1, 0] = load_xq(1, 0)
+        load_scales(ws_plane, ws_scales)
+        raw[1, 1] = load_xq(1, 1)
+        load_scales(wa_plane, wa_scales)
+        wq = load_words("wq", wq_words)
+        load_scales(wq_plane, wq_scales)
+
+        xq_codes = [keep.tile([P, T], U32, name="xq_codes_%d" % z, align_bytes=64) for z in range(2)]
+        xq_plane = [keep.tile([P, T], U8, name="xq_plane_%d" % z, align_bytes=64) for z in range(2)]
+        for z in range(2):
+            for h in range(2):
+                grouped = [
+                    keep.tile([P, QUARTER, PACK], BF16, name="grouped_%d_%d_%d" % (z, h, e), align_bytes=64)
+                    for e in range(2)
+                ]
+                for e, copy in enumerate((nc.vector.tensor_copy, nc.scalar.copy)):
+                    src = raw[z, h][:, :, e * QUARTER : (e + 1) * QUARTER]
+                    copy(
+                        out=grouped[e][:].rearrange("p (c i) j -> p c j i", i=4),
+                        in_=src.rearrange("p j (c i) -> p c j i", i=4),
+                    )
+                for e in range(2):
+                    cols = slice(h * HALF + e * QUARTER, h * HALF + (e + 1) * QUARTER)
+                    nc.vector.quantize_mx(
+                        out=xq_codes[z][:, cols].bitcast(FP8X4),
+                        scales=xq_plane[z][:, cols],
+                        in_=grouped[e][:].rearrange("p c j -> p (c j)"),
+                    )
+
+        r_acc = [psum.tile([P, T], F32, name="r_acc_%d" % i) for i in range(N_TILES)]
+        p_acc = [psum.tile([P, T], F32, name="p_acc_%d" % i) for i in range(N_TILES)]
+        xt_operand = (xt[:].bitcast(FP8X4), xt_plane[:])
+        xq_operand = [(xq_codes[z][:].bitcast(FP8X4), xq_plane[z][:]) for z in range(2)]
+
+        def mx_pass(acc, codes, plane, dtype, column_bytes, z, i, moving, start, stop):
+            first = z * N + i * P
+            nc.tensor.matmul_mx(
+                out=acc[:],
+                lhsT=codes[:, first * column_bytes : (first + P) * column_bytes].bitcast(dtype),
+                lhsT_scale=plane[:, first : first + P],
+                rhs=moving[0],
+                rhs_scale=moving[1],
+                start=start,
+                stop=stop,
+            )
+
+        for i in range(N_TILES):
+            mx_pass(r_acc[i], wb, wb_plane, FP8X4, 4, 0, i, xt_operand, True, False)
+        for i in range(N_TILES):
+            mx_pass(r_acc[i], ws, ws_plane, FP4X4, 2, 0, i, xq_operand[0], False, False)
+        for i in range(N_TILES):
+            mx_pass(p_acc[i], wa, wa_plane, FP4X4, 2, 0, i, xt_operand, True, False)
+        for i in range(N_TILES):
+            mx_pass(r_acc[i], ws, ws_plane, FP4X4, 2, 1, i, xq_operand[1], False, True)
+            mx_pass(p_acc[i], wq, wq_plane, FP4X4, 2, 0, i, xq_operand[0], False, False)
+            mx_pass(p_acc[i], wq, wq_plane, FP4X4, 2, 1, i, xq_operand[1], False, True)
+
+        halves = [slice(h * HALF, (h + 1) * HALF) for h in range(2)]
+        for i in range(N_TILES):
+            mag = keep.tile([P, T], F32, name="mag_%d" % i)
+            root = keep.tile([P, T], F32, name="root_%d" % i)
+            r_root = keep.tile([P, T], F32, name="r_root_%d" % i)
+            p_root = keep.tile([P, T], F32, name="p_root_%d" % i)
+            result = keep.tile([P, T], F32, name="result_%d" % i)
+            for cols in halves:
+                nc.scalar.activation(out=mag[:, cols], in_=r_acc[i][:, cols], func=ACT.Abs)
+            for cols in halves:
+                nc.scalar.activation(out=root[:, cols], in_=mag[:, cols], func=ACT.Abs_reciprocal_sqrt, bias=1.0)
+            for cols in halves:
+                nc.vector.tensor_tensor(out=r_root[:, cols], in0=r_acc[i][:, cols], in1=root[:, cols], op=ALU.mult)
+                nc.vector.tensor_tensor(out=p_root[:, cols], in0=p_acc[i][:, cols], in1=root[:, cols], op=ALU.mult)
+                nc.gpsimd.tensor_tensor(out=result[:, cols], in0=r_root[:, cols], in1=p_root[:, cols], op=ALU.mult)
+            nc.sync.dma_start(out=out[i * P : (i + 1) * P, :], in_=result[:])

@@ -32,16 +32,16 @@ def tile_mix_product_of_two_sums_kernel(
         psum = ctx.enter_context(tc.psum_pool(name="psum", bufs=1))
         ctx.enter_context(tc.manual_schedule())
 
-        def plane_tile(name, passes):
+        def plane_tile(engine, name, passes):
             plane = keep.tile([P, passes * N], U8, name=name, align_bytes=64)
-            nc.vector.memset(plane[:].bitcast(I32), 0)
+            engine.memset(plane[:].bitcast(I32), 0)
             return plane
 
-        def load_scales(plane, scales):
+        def load_scales(queue, plane, scales, which):
             passes = scales.shape[0]
             rows = scales.bitcast(I32).rearrange("z (q r) c -> r q z c", r=4)
-            for r in range(4):
-                nc.sync.dma_start(
+            for r in which:
+                queue.dma_start(
                     out=plane[:].bitcast(I32)[r:P:32, :].rearrange("q (z c) -> q z c", z=passes), in_=rows[r]
                 )
 
@@ -60,28 +60,35 @@ def tile_mix_product_of_two_sums_kernel(
             nc.sync.dma_start(out=raw[:], in_=rows.rearrange("(p j) w -> p j w", j=PACK))
             return raw
 
+        xt_plane = plane_tile(nc.gpsimd, "xt_plane", 1)
+        wa_plane = plane_tile(nc.gpsimd, "wa_plane", 1)
+        wb_plane = plane_tile(nc.vector, "wb_plane", 1)
+        ws_plane = plane_tile(nc.vector, "ws_plane", 2)
+        wq_plane = plane_tile(nc.vector, "wq_plane", 2)
 
-        xt_plane = plane_tile("xt_plane", 1)
-        wb_plane = plane_tile("wb_plane", 1)
-        ws_plane = plane_tile("ws_plane", 2)
-        wa_plane = plane_tile("wa_plane", 1)
-        wq_plane = plane_tile("wq_plane", 2)
+        warm_in = keep.tile([P, 1], F32, name="warm_in")
+        warm_out = keep.tile([P, 1], F32, name="warm_out")
+        nc.vector.memset(warm_in[:], 1.0)
+        nc.scalar.activation(out=warm_out[:], in_=warm_in[:], func=ACT.Abs_reciprocal_sqrt)
 
         raw = {}
+        load_scales(nc.gpsimd, wa_plane, wa_scales, (0, 1, 2, 3,))
         raw[0, 0] = load_xq(0, 0)
+        load_scales(nc.sync, xt_plane, xt_scales, (0, 1,))
         xt = load_words("xt", xt_words.rearrange("z p c r -> z p (c r)"))
+        load_scales(nc.sync, xt_plane, xt_scales, (2, 3,))
         wb = load_words("wb", wb_words.rearrange("z p c r -> z p (c r)"))
-        load_scales(xt_plane, xt_scales)
+        load_scales(nc.sync, wb_plane, wb_scales, (0,))
         raw[0, 1] = load_xq(0, 1)
-        load_scales(wb_plane, wb_scales)
-        wa = load_words("wa", wa_words)
+        load_scales(nc.sync, wb_plane, wb_scales, (1, 2, 3,))
         ws = load_words("ws", ws_words)
+        load_scales(nc.sync, ws_plane, ws_scales, (0, 1,))
         raw[1, 0] = load_xq(1, 0)
-        load_scales(ws_plane, ws_scales)
+        load_scales(nc.sync, ws_plane, ws_scales, (2, 3,))
         raw[1, 1] = load_xq(1, 1)
-        load_scales(wa_plane, wa_scales)
+        wa = load_words("wa", wa_words)
         wq = load_words("wq", wq_words)
-        load_scales(wq_plane, wq_scales)
+        load_scales(nc.sync, wq_plane, wq_scales, (0, 1, 2, 3,))
 
         xq_codes = [keep.tile([P, T], U32, name="xq_codes_%d" % z, align_bytes=64) for z in range(2)]
         xq_plane = [keep.tile([P, T], U8, name="xq_plane_%d" % z, align_bytes=64) for z in range(2)]
@@ -122,30 +129,46 @@ def tile_mix_product_of_two_sums_kernel(
                 stop=stop,
             )
 
+        def close_r(i):
+            mx_pass(r_acc[i], ws, ws_plane, FP4X4, 2, 1, i, xq_operand[1], False, True)
+
+        def all_of_p(i):
+            mx_pass(p_acc[i], wa, wa_plane, FP4X4, 2, 0, i, xt_operand, True, False)
+            mx_pass(p_acc[i], wq, wq_plane, FP4X4, 2, 0, i, xq_operand[0], False, False)
+            mx_pass(p_acc[i], wq, wq_plane, FP4X4, 2, 1, i, xq_operand[1], False, True)
+
         for i in range(N_TILES):
             mx_pass(r_acc[i], wb, wb_plane, FP8X4, 4, 0, i, xt_operand, True, False)
         for i in range(N_TILES):
             mx_pass(r_acc[i], ws, ws_plane, FP4X4, 2, 0, i, xq_operand[0], False, False)
+        close_r(0)
         for i in range(N_TILES):
-            mx_pass(p_acc[i], wa, wa_plane, FP4X4, 2, 0, i, xt_operand, True, False)
-        for i in range(N_TILES):
-            mx_pass(r_acc[i], ws, ws_plane, FP4X4, 2, 1, i, xq_operand[1], False, True)
-            mx_pass(p_acc[i], wq, wq_plane, FP4X4, 2, 0, i, xq_operand[0], False, False)
-            mx_pass(p_acc[i], wq, wq_plane, FP4X4, 2, 1, i, xq_operand[1], False, True)
+            if i + 1 < N_TILES:
+                close_r(i + 1)
+            all_of_p(i)
 
         halves = [slice(h * HALF, (h + 1) * HALF) for h in range(2)]
         for i in range(N_TILES):
             mag = keep.tile([P, T], F32, name="mag_%d" % i)
             root = keep.tile([P, T], F32, name="root_%d" % i)
-            r_root = keep.tile([P, T], F32, name="r_root_%d" % i)
-            p_root = keep.tile([P, T], F32, name="p_root_%d" % i)
+            r_part = keep.tile([P, T], F32, name="r_part_%d" % i)
+            p_part = keep.tile([P, T], F32, name="p_part_%d" % i)
             result = keep.tile([P, T], F32, name="result_%d" % i)
             for cols in halves:
                 nc.scalar.activation(out=mag[:, cols], in_=r_acc[i][:, cols], func=ACT.Abs)
             for cols in halves:
                 nc.scalar.activation(out=root[:, cols], in_=mag[:, cols], func=ACT.Abs_reciprocal_sqrt, bias=1.0)
-            for cols in halves:
-                nc.vector.tensor_tensor(out=r_root[:, cols], in0=r_acc[i][:, cols], in1=root[:, cols], op=ALU.mult)
-                nc.vector.tensor_tensor(out=p_root[:, cols], in0=p_acc[i][:, cols], in1=root[:, cols], op=ALU.mult)
-                nc.gpsimd.tensor_tensor(out=result[:, cols], in0=r_root[:, cols], in1=p_root[:, cols], op=ALU.mult)
-            nc.sync.dma_start(out=out[i * P : (i + 1) * P, :], in_=result[:])
+            if i < 3:
+                for cols in halves:
+                    nc.vector.tensor_tensor(out=r_part[:, cols], in0=r_acc[i][:, cols], in1=root[:, cols], op=ALU.mult)
+                    nc.vector.tensor_tensor(out=p_part[:, cols], in0=p_acc[i][:, cols], in1=root[:, cols], op=ALU.mult)
+                    nc.gpsimd.tensor_tensor(out=result[:, cols], in0=r_part[:, cols], in1=p_part[:, cols], op=ALU.mult)
+                nc.sync.dma_start(out=out[i * P : (i + 1) * P, :], in_=result[:])
+            else:
+                for cols in halves:
+                    nc.scalar.activation(out=p_part[:, cols], in_=root[:, cols], func=ACT.Square)
+                for cols in halves:
+                    nc.vector.tensor_tensor(out=r_part[:, cols], in0=r_acc[i][:, cols], in1=p_part[:, cols], op=ALU.mult)
+                for cols in halves:
+                    nc.vector.tensor_tensor(out=result[:, cols], in0=p_acc[i][:, cols], in1=r_part[:, cols], op=ALU.mult)
+                    nc.sync.dma_start(out=out[i * P : (i + 1) * P, cols], in_=result[:, cols])

@@ -20,7 +20,9 @@ PACK = 4
 PASS = P * PACK
 N_TILES = N // P
 HALF = T // 2
-QUARTER = T // 4
+R_LEAD = 2
+SHARE = T // 4
+GPSIMD_HALVES = 5
 
 
 def tile_mix_product_of_two_sums_kernel(
@@ -54,62 +56,56 @@ def tile_mix_product_of_two_sums_kernel(
             )
             return codes
 
-        def load_xq(z, h):
-            raw = keep.tile([P, PACK, HALF], F32, name="xq_raw_%d_%d" % (z, h))
-            rows = xq[z * PASS : (z + 1) * PASS, h * HALF : (h + 1) * HALF]
+        def load_xq(z, first, width):
+            raw = keep.tile([P, PACK, width], F32, name="xq_raw_%d_%d" % (z, first))
+            rows = xq[z * PASS : (z + 1) * PASS, first : first + width]
             nc.sync.dma_start(out=raw[:], in_=rows.rearrange("(p j) w -> p j w", j=PACK))
-            return raw
+            pieces.append((z, first, width, raw))
 
         xt_plane = plane_tile(nc.gpsimd, "xt_plane", 1)
-        wa_plane = plane_tile(nc.gpsimd, "wa_plane", 1)
-        wb_plane = plane_tile(nc.vector, "wb_plane", 1)
         ws_plane = plane_tile(nc.vector, "ws_plane", 2)
+        wb_plane = plane_tile(nc.vector, "wb_plane", 1)
         wq_plane = plane_tile(nc.vector, "wq_plane", 2)
+        wa_plane = plane_tile(nc.vector, "wa_plane", 1)
 
         warm_in = keep.tile([P, 1], F32, name="warm_in")
         warm_out = keep.tile([P, 1], F32, name="warm_out")
         nc.vector.memset(warm_in[:], 1.0)
         nc.scalar.activation(out=warm_out[:], in_=warm_in[:], func=ACT.Abs_reciprocal_sqrt)
 
-        raw = {}
-        load_scales(nc.gpsimd, wa_plane, wa_scales, (0, 1, 2, 3,))
-        raw[0, 0] = load_xq(0, 0)
-        load_scales(nc.sync, xt_plane, xt_scales, (0, 1,))
-        xt = load_words("xt", xt_words.rearrange("z p c r -> z p (c r)"))
-        load_scales(nc.sync, xt_plane, xt_scales, (2, 3,))
-        wb = load_words("wb", wb_words.rearrange("z p c r -> z p (c r)"))
-        load_scales(nc.sync, wb_plane, wb_scales, (0,))
-        raw[0, 1] = load_xq(0, 1)
-        load_scales(nc.sync, wb_plane, wb_scales, (1, 2, 3,))
+        pieces = []
+        load_scales(nc.gpsimd, xt_plane, xt_scales, (0, 1, 2, 3,))
+        load_xq(0, 0, 512)
         ws = load_words("ws", ws_words)
-        load_scales(nc.sync, ws_plane, ws_scales, (0, 1,))
-        raw[1, 0] = load_xq(1, 0)
-        load_scales(nc.sync, ws_plane, ws_scales, (2, 3,))
-        raw[1, 1] = load_xq(1, 1)
-        wa = load_words("wa", wa_words)
-        wq = load_words("wq", wq_words)
+        load_scales(nc.sync, ws_plane, ws_scales, (0, 1, 2, 3,))
+        load_xq(1, 0, 256)
+        load_xq(1, 256, 256)
+        load_scales(nc.sync, wb_plane, wb_scales, (0, 1, 2, 3,))
+        xt = load_words("xt", xt_words.rearrange("z p c r -> z p (c r)"))
+        wb = load_words("wb", wb_words.rearrange("z p c r -> z p (c r)"))
         load_scales(nc.sync, wq_plane, wq_scales, (0, 1, 2, 3,))
+        wq = load_words("wq", wq_words)
+        wa = load_words("wa", wa_words)
+        load_scales(nc.sync, wa_plane, wa_scales, (0, 1, 2, 3,))
 
         xq_codes = [keep.tile([P, T], U32, name="xq_codes_%d" % z, align_bytes=64) for z in range(2)]
         xq_plane = [keep.tile([P, T], U8, name="xq_plane_%d" % z, align_bytes=64) for z in range(2)]
-        for z in range(2):
-            for h in range(2):
-                grouped = [
-                    keep.tile([P, QUARTER, PACK], BF16, name="grouped_%d_%d_%d" % (z, h, e), align_bytes=64)
-                    for e in range(2)
-                ]
+        for z, first, width, raw in pieces:
+            for start in range(0, width, HALF):
+                grouped = []
                 for e, copy in enumerate((nc.vector.tensor_copy, nc.scalar.copy)):
-                    src = raw[z, h][:, :, e * QUARTER : (e + 1) * QUARTER]
+                    offset = start + e * SHARE
+                    part = keep.tile([P, SHARE, PACK], BF16, name="grouped_%d_%d" % (z, first + offset), align_bytes=64)
                     copy(
-                        out=grouped[e][:].rearrange("p (c i) j -> p c j i", i=4),
-                        in_=src.rearrange("p j (c i) -> p c j i", i=4),
+                        out=part[:].rearrange("p (c i) j -> p c j i", i=4),
+                        in_=raw[:, :, offset : offset + SHARE].rearrange("p j (c i) -> p c j i", i=4),
                     )
-                for e in range(2):
-                    cols = slice(h * HALF + e * QUARTER, h * HALF + (e + 1) * QUARTER)
+                    grouped.append((part, slice(first + offset, first + offset + SHARE)))
+                for part, cols in grouped:
                     nc.vector.quantize_mx(
                         out=xq_codes[z][:, cols].bitcast(FP8X4),
                         scales=xq_plane[z][:, cols],
-                        in_=grouped[e][:].rearrange("p c j -> p (c j)"),
+                        in_=part[:].rearrange("p c j -> p (c j)"),
                     )
 
         r_acc = [psum.tile([P, T], F32, name="r_acc_%d" % i) for i in range(N_TILES)]
@@ -130,22 +126,21 @@ def tile_mix_product_of_two_sums_kernel(
             )
 
         def close_r(i):
-            mx_pass(r_acc[i], ws, ws_plane, FP4X4, 2, 1, i, xq_operand[1], False, True)
+            mx_pass(r_acc[i], ws, ws_plane, FP4X4, 2, 1, i, xq_operand[1], False, False)
+            mx_pass(r_acc[i], wb, wb_plane, FP8X4, 4, 0, i, xt_operand, False, True)
 
         def all_of_p(i):
-            mx_pass(p_acc[i], wa, wa_plane, FP4X4, 2, 0, i, xt_operand, True, False)
-            mx_pass(p_acc[i], wq, wq_plane, FP4X4, 2, 0, i, xq_operand[0], False, False)
-            mx_pass(p_acc[i], wq, wq_plane, FP4X4, 2, 1, i, xq_operand[1], False, True)
+            mx_pass(p_acc[i], wq, wq_plane, FP4X4, 2, 0, i, xq_operand[0], True, False)
+            mx_pass(p_acc[i], wq, wq_plane, FP4X4, 2, 1, i, xq_operand[1], False, False)
+            mx_pass(p_acc[i], wa, wa_plane, FP4X4, 2, 0, i, xt_operand, False, True)
 
         for i in range(N_TILES):
-            mx_pass(r_acc[i], wb, wb_plane, FP8X4, 4, 0, i, xt_operand, True, False)
-        for i in range(N_TILES):
-            mx_pass(r_acc[i], ws, ws_plane, FP4X4, 2, 0, i, xq_operand[0], False, False)
-        close_r(0)
-        for i in range(N_TILES):
-            if i + 1 < N_TILES:
-                close_r(i + 1)
-            all_of_p(i)
+            mx_pass(r_acc[i], ws, ws_plane, FP4X4, 2, 0, i, xq_operand[0], True, False)
+        for i in range(N_TILES + R_LEAD):
+            if i < N_TILES:
+                close_r(i)
+            if i >= R_LEAD:
+                all_of_p(i - R_LEAD)
 
         halves = [slice(h * HALF, (h + 1) * HALF) for h in range(2)]
         for i in range(N_TILES):
@@ -158,17 +153,19 @@ def tile_mix_product_of_two_sums_kernel(
                 nc.scalar.activation(out=mag[:, cols], in_=r_acc[i][:, cols], func=ACT.Abs)
             for cols in halves:
                 nc.scalar.activation(out=root[:, cols], in_=mag[:, cols], func=ACT.Abs_reciprocal_sqrt, bias=1.0)
-            if i < 3:
-                for cols in halves:
-                    nc.vector.tensor_tensor(out=r_part[:, cols], in0=r_acc[i][:, cols], in1=root[:, cols], op=ALU.mult)
-                    nc.vector.tensor_tensor(out=p_part[:, cols], in0=p_acc[i][:, cols], in1=root[:, cols], op=ALU.mult)
-                    nc.gpsimd.tensor_tensor(out=result[:, cols], in0=r_part[:, cols], in1=p_part[:, cols], op=ALU.mult)
-                nc.sync.dma_start(out=out[i * P : (i + 1) * P, :], in_=result[:])
-            else:
-                for cols in halves:
-                    nc.scalar.activation(out=p_part[:, cols], in_=root[:, cols], func=ACT.Square)
-                for cols in halves:
-                    nc.vector.tensor_tensor(out=r_part[:, cols], in0=r_acc[i][:, cols], in1=p_part[:, cols], op=ALU.mult)
-                for cols in halves:
-                    nc.vector.tensor_tensor(out=result[:, cols], in0=p_acc[i][:, cols], in1=r_part[:, cols], op=ALU.mult)
-                    nc.sync.dma_start(out=out[i * P : (i + 1) * P, cols], in_=result[:, cols])
+            on_gpsimd = halves[: max(0, min(2, GPSIMD_HALVES - 2 * i))]
+            on_scalar = halves[len(on_gpsimd) :]
+            for cols in on_scalar:
+                nc.scalar.activation(out=p_part[:, cols], in_=root[:, cols], func=ACT.Square)
+            if on_gpsimd:
+                cols = slice(0, on_gpsimd[-1].stop)
+                nc.vector.tensor_tensor(out=r_part[:, cols], in0=r_acc[i][:, cols], in1=root[:, cols], op=ALU.mult)
+            for cols in on_scalar:
+                nc.vector.tensor_tensor(out=r_part[:, cols], in0=r_acc[i][:, cols], in1=p_part[:, cols], op=ALU.mult)
+            for cols in on_gpsimd:
+                nc.vector.tensor_tensor(out=p_part[:, cols], in0=p_acc[i][:, cols], in1=root[:, cols], op=ALU.mult)
+                nc.gpsimd.tensor_tensor(out=result[:, cols], in0=r_part[:, cols], in1=p_part[:, cols], op=ALU.mult)
+            for cols in on_scalar:
+                nc.vector.tensor_tensor(out=result[:, cols], in0=p_acc[i][:, cols], in1=r_part[:, cols], op=ALU.mult)
+            for cols in on_scalar + on_gpsimd if on_scalar else [slice(0, T)]:
+                nc.sync.dma_start(out=out[i * P : (i + 1) * P, cols], in_=result[:, cols])

from contextlib import ExitStack

import concourse.mybir as mybir

K, L, T, N = 512, 1024, 512, 512
FLOPS = 2 * 2 * (K + L) * T * N

F32 = mybir.dt.float32
BF16 = mybir.dt.bfloat16
I32 = mybir.dt.int32
U32 = mybir.dt.uint32
U8 = mybir.dt.uint8
FP8X4 = mybir.dt.float8_e4m3fn_x4
FP4X4 = mybir.dt.float4_e2m1fn_x4
ACT = mybir.ActivationFunctionType
ALU = mybir.AluOpType

P = 128
PACK = 4
PASS = P * PACK
N_TILES = N // P
HALF = T // 2
R_LEAD = 2
SHARE = T // 4
GPSIMD_HALVES = 5


def tile_mix_product_of_two_sums_kernel(
    tc, xt_words, xt_scales, wa_words, wa_scales, xq, wq_words, wq_scales, wb_words, wb_scales, ws_words, ws_scales, out
):
    nc = tc.nc
    with ExitStack() as ctx:
        keep = ctx.enter_context(tc.tile_pool(name="keep", bufs=1))
        psum = ctx.enter_context(tc.psum_pool(name="psum", bufs=1))
        ctx.enter_context(tc.manual_schedule())

        def plane_tile(engine, name, passes):
            plane = keep.tile([P, passes * N], U8, name=name, align_bytes=64)
            engine.memset(plane[:].bitcast(I32), 0)
            return plane

        def load_scales(queue, plane, scales, which):
            passes = scales.shape[0]
            rows = scales.bitcast(I32).rearrange("z (q r) c -> r q z c", r=4)
            for r in which:
                queue.dma_start(
                    out=plane[:].bitcast(I32)[r:P:32, :].rearrange("q (z c) -> q z c", z=passes), in_=rows[r]
                )

        def load_words(name, words):
            passes, width = words.shape[0], words.shape[2]
            codes = keep.tile([P, passes * width], U8, name=name, align_bytes=64)
            nc.sync.dma_start(
                out=codes[:].bitcast(I32).rearrange("p (z c) -> p z c", z=passes),
                in_=words.bitcast(I32).rearrange("z p c -> p z c"),
            )
            return codes

        def load_xq(z, first, width):
            raw = keep.tile([P, PACK, width], F32, name="xq_raw_%d_%d" % (z, first))
            rows = xq[z * PASS : (z + 1) * PASS, first : first + width]
            nc.sync.dma_start(out=raw[:], in_=rows.rearrange("(p j) w -> p j w", j=PACK))
            pieces.append((z, first, width, raw))

        xt_plane = plane_tile(nc.gpsimd, "xt_plane", 1)
        ws_plane = plane_tile(nc.vector, "ws_plane", 2)
        wb_plane = plane_tile(nc.vector, "wb_plane", 1)
        wq_plane = plane_tile(nc.vector, "wq_plane", 2)
        wa_plane = plane_tile(nc.vector, "wa_plane", 1)

        warm_in = keep.tile([P, 1], F32, name="warm_in")
        warm_out = keep.tile([P, 1], F32, name="warm_out")
        nc.vector.memset(warm_in[:], 1.0)
        nc.scalar.activation(out=warm_out[:], in_=warm_in[:], func=ACT.Abs_reciprocal_sqrt)

        pieces = []
        load_scales(nc.gpsimd, xt_plane, xt_scales, (0, 1, 2, 3,))
        load_xq(0, 0, 512)
        ws = load_words("ws", ws_words)
        load_scales(nc.sync, ws_plane, ws_scales, (0, 1, 2, 3,))
        load_xq(1, 0, 256)
        load_xq(1, 256, 256)
        load_scales(nc.sync, wb_plane, wb_scales, (0, 1, 2, 3,))
        xt = load_words("xt", xt_words.rearrange("z p c r -> z p (c r)"))
        wb = load_words("wb", wb_words.rearrange("z p c r -> z p (c r)"))
        load_scales(nc.sync, wq_plane, wq_scales, (0, 1, 2, 3,))
        wq = load_words("wq", wq_words)
        wa = load_words("wa", wa_words)
        load_scales(nc.sync, wa_plane, wa_scales, (0, 1, 2, 3,))

        xq_codes = [keep.tile([P, T], U32, name="xq_codes_%d" % z, align_bytes=64) for z in range(2)]
        xq_plane = [keep.tile([P, T], U8, name="xq_plane_%d" % z, align_bytes=64) for z in range(2)]
        for z, first, width, raw in pieces:
            for start in range(0, width, HALF):
                grouped = []
                for e, copy in enumerate((nc.vector.tensor_copy, nc.scalar.copy)):
                    offset = start + e * SHARE
                    part = keep.tile([P, SHARE, PACK], BF16, name="grouped_%d_%d" % (z, first + offset), align_bytes=64)
                    copy(
                        out=part[:].rearrange("p (c i) j -> p c j i", i=4),
                        in_=raw[:, :, offset : offset + SHARE].rearrange("p j (c i) -> p c j i", i=4),
                    )
                    grouped.append((part, slice(first + offset, first + offset + SHARE)))
                for part, cols in grouped:
                    nc.vector.quantize_mx(
                        out=xq_codes[z][:, cols].bitcast(FP8X4),
                        scales=xq_plane[z][:, cols],
                        in_=part[:].rearrange("p c j -> p (c j)"),
                    )

        r_acc = [psum.tile([P, T], F32, name="r_acc_%d" % i) for i in range(N_TILES)]
        p_acc = [psum.tile([P, T], F32, name="p_acc_%d" % i) for i in range(N_TILES)]
        xt_operand = (xt[:].bitcast(FP8X4), xt_plane[:])
        xq_operand = [(xq_codes[z][:].bitcast(FP8X4), xq_plane[z][:]) for z in range(2)]

        def mx_pass(acc, codes, plane, dtype, column_bytes, z, i, moving, start, stop):
            first = z * N + i * P
            nc.tensor.matmul_mx(
                out=acc[:],
                lhsT=codes[:, first * column_bytes : (first + P) * column_bytes].bitcast(dtype),
                lhsT_scale=plane[:, first : first + P],
                rhs=moving[0],
                rhs_scale=moving[1],
                start=start,
                stop=stop,
            )

        def close_r(i):
            mx_pass(r_acc[i], ws, ws_plane, FP4X4, 2, 1, i, xq_operand[1], False, False)
            mx_pass(r_acc[i], wb, wb_plane, FP8X4, 4, 0, i, xt_operand, False, True)

        def all_of_p(i):
            mx_pass(p_acc[i], wq, wq_plane, FP4X4, 2, 0, i, xq_operand[0], True, False)
            mx_pass(p_acc[i], wq, wq_plane, FP4X4, 2, 1, i, xq_operand[1], False, False)
            mx_pass(p_acc[i], wa, wa_plane, FP4X4, 2, 0, i, xt_operand, False, True)

        for i in range(N_TILES):
            mx_pass(r_acc[i], ws, ws_plane, FP4X4, 2, 0, i, xq_operand[0], True, False)
        for i in range(N_TILES + R_LEAD):
            if i < N_TILES:
                close_r(i)
            if i >= R_LEAD:
                all_of_p(i - R_LEAD)

        halves = [slice(h * HALF, (h + 1) * HALF) for h in range(2)]
        for i in range(N_TILES):
            mag = keep.tile([P, T], F32, name="mag_%d" % i)
            root = keep.tile([P, T], F32, name="root_%d" % i)
            r_part = keep.tile([P, T], F32, name="r_part_%d" % i)
            p_part = keep.tile([P, T], F32, name="p_part_%d" % i)
            result = keep.tile([P, T], F32, name="result_%d" % i)
            for cols in halves:
                nc.scalar.activation(out=mag[:, cols], in_=r_acc[i][:, cols], func=ACT.Abs)
            for cols in halves:
                nc.scalar.activation(out=root[:, cols], in_=mag[:, cols], func=ACT.Abs_reciprocal_sqrt, bias=1.0)
            on_gpsimd = halves[: max(0, min(2, GPSIMD_HALVES - 2 * i))]
            on_scalar = halves[len(on_gpsimd) :]
            for cols in on_scalar:
                nc.scalar.activation(out=p_part[:, cols], in_=root[:, cols], func=ACT.Square)
            if on_gpsimd:
                cols = slice(0, on_gpsimd[-1].stop)
                nc.vector.tensor_tensor(out=r_part[:, cols], in0=r_acc[i][:, cols], in1=root[:, cols], op=ALU.mult)
            for cols in on_scalar:
                nc.vector.tensor_tensor(out=r_part[:, cols], in0=r_acc[i][:, cols], in1=p_part[:, cols], op=ALU.mult)
            for cols in on_gpsimd:
                nc.vector.tensor_tensor(out=p_part[:, cols], in0=p_acc[i][:, cols], in1=root[:, cols], op=ALU.mult)
                nc.gpsimd.tensor_tensor(out=result[:, cols], in0=r_part[:, cols], in1=p_part[:, cols], op=ALU.mult)
            for cols in on_scalar:
                nc.vector.tensor_tensor(out=result[:, cols], in0=p_acc[i][:, cols], in1=r_part[:, cols], op=ALU.mult)
            for cols in on_scalar + on_gpsimd if on_scalar else [slice(0, T)]:
                nc.sync.dma_start(out=out[i * P : (i + 1) * P, cols], in_=result[:, cols])
